import numpy as np
import ml_dtypes


def mxq(x, axis, fmt="e4m3"):
    dtype, down = {"e4m3": (ml_dtypes.float8_e4m3fn, 7), "e5m2": (ml_dtypes.float8_e5m2, 14)}[fmt]
    v = np.moveaxis(np.asarray(x, np.float32).astype(ml_dtypes.bfloat16).astype(np.float64), axis, -1)
    blocks = v.reshape(v.shape[:-1] + (-1, 32))
    amax = np.abs(blocks).max(-1, keepdims=True)
    byte = np.maximum(np.where(amax > 0, np.frexp(amax)[1] - 1 + 127, 0) - down, 1)
    scale = np.exp2(byte - 127.0)
    codes = (blocks / scale).astype(np.float32).astype(dtype).astype(np.float64)
    return np.moveaxis((codes * scale).reshape(v.shape), -1, axis)


WIDE = False


def mx_kscale(k):
    if not WIDE:
        return np.ones(k)
    levels = np.array([10, -10, 5, -5, 0])
    if k % 512:
        return np.exp2(np.random.permutation(np.resize(levels, k // 32))).repeat(32)
    a = np.empty((k // 512, 16))
    for p in range(k // 512):
        a[p, :8] = np.random.permutation(np.resize(levels, 8))
        for g in range(8):
            far = levels[np.abs(levels - a[p, g]) >= 10]
            a[p, g + 8] = far[np.random.randint(len(far))]
    return np.exp2(a.ravel()).repeat(32)


def f64(x):
    return np.asarray(x).astype(np.float64)


def striped(idx):
    return np.tile(idx.reshape(-1, 16).T, (8, 1)).astype(np.uint16)


def unstriped(offs):
    return offs[:16].T.reshape(-1).astype(np.int64)


E2M1 = np.array([0.0, 0.5, 1.0, 1.5, 2.0, 3.0, 4.0, 6.0, -0.0, -0.5, -1.0, -1.5, -2.0, -3.0, -4.0, -6.0])


def pack_weight(w, fmt):
    k, n = w.shape
    w = f64(np.asarray(w, np.float32).astype(ml_dtypes.bfloat16)).reshape(k // 32, 32, n)
    amax = np.abs(w).max(1)
    if fmt == "e4m3":
        byte = np.frexp(amax)[1] - 1 + 127 - 7
    else:
        mant, ex = np.frexp(amax / 6.0)
        byte = np.where(mant > 0.5, ex, ex - 1) + 127
    byte = np.clip(np.where(amax > 0, byte, 1), 1, 254)
    scaled = (w * np.exp2(127.0 - byte)[:, None, :]).reshape(k, n).astype(np.float32)
    by_word = np.ascontiguousarray(scaled.reshape(k // 512, 128, 4, n).transpose(0, 1, 3, 2))
    if fmt == "e4m3":
        words = by_word.astype(ml_dtypes.float8_e4m3fn).view(np.uint8)
    else:
        c = by_word.astype(ml_dtypes.float4_e2m1fn).view(np.uint8) & 0xF
        words = (c[..., 0::2] | (c[..., 1::2] << 4)).reshape(k // 512, 128, 2 * n)
    return np.ascontiguousarray(words), np.ascontiguousarray(byte.astype(np.uint8).reshape(k // 512, 16, n))


def unpack_weight(words, scales, fmt):
    g, _, n = scales.shape
    words = np.ascontiguousarray(words).reshape(g, 128, n, -1)
    if fmt == "e4m3":
        vals = words.view(ml_dtypes.float8_e4m3fn).astype(np.float64)
    else:
        nib = np.empty((g, 128, n, 4), np.uint8)
        nib[..., 0::2] = words & 0xF
        nib[..., 1::2] = words >> 4
        vals = E2M1[nib]
    vals = vals * np.repeat(np.exp2(scales.astype(np.float64) - 127.0), 8, axis=1)[..., None]
    return vals.transpose(0, 1, 3, 2).reshape(g * 512, n)


def gelu(v):
    return 0.5 * v * (1.0 + np.tanh(np.sqrt(2.0 / np.pi) * (v + 0.044715 * v**3)))


K, H, N, T, S, T2 = 1024, 512, 512, 4096, 1024, 2048


def setup_inputs():
    n = np.random.standard_normal
    s = mx_kscale(K)[:, None]
    u = mx_kscale(H)[:, None]
    tab_words, tab_scales = pack_weight(n((K, T)) * s, "e4m3")
    wa_words, wa_scales = pack_weight(n((K, H)) * 1.2 / np.sqrt(K) / s, "e2m1")
    wb = (n((K, H)) * 0.53 / np.sqrt(K) / s).astype(np.float32)
    gain = (np.exp(0.3 * n(H)) * u[:, 0]).astype(np.float32)
    wc = (n((H, N)) * 1.5 / np.sqrt(H) / u).astype(np.float32)
    lane = np.exp(0.4 * n((N, S))).astype(np.float32)
    wgo = np.exp(0.3 * n((128, S))).astype(np.float32)
    offs = striped(np.random.permutation(T)[:S])
    offs2 = striped(np.random.permutation(T)[:S])
    offs3 = striped(np.random.permutation(T2)[:S])
    return {"tab_words": tab_words, "tab_scales": tab_scales,
            "offs": offs, "offs2": offs2, "offs3": offs3,
            "wa_words": wa_words, "wa_scales": wa_scales,
            "wb": wb, "gain": gain, "wc": wc, "lane": lane, "wgo": wgo}


def reference(tab_words, tab_scales, offs, offs2, offs3, wa_words, wa_scales,
              wb, gain, wc, lane, wgo):
    TW = unpack_weight(tab_words, tab_scales, "e4m3")
    v = TW[:, unstriped(offs)]
    v2 = TW[:, unstriped(offs2)]
    wa = unpack_weight(wa_words, wa_scales, "e2m1")
    ship = np.tanh(wa.T @ v)
    truck = np.sin(mxq(f64(wb), 0, "e4m3").T @ v2)
    z = f64(gain)[:, None] * np.minimum(ship, truck)
    y = mxq(f64(wc), 0, "e4m3").T @ mxq(z, 0, "e4m3")
    y = f64(lane) * y
    out = np.zeros((N, T2))
    out[:, unstriped(offs3)] = np.tile(f64(wgo), (N // 128, 1)) * y
    return out

@@ -1,0 +1,249 @@
+from contextlib import ExitStack
+
+import concourse.mybir as mybir
+
+K, H, N, T, S, T2 = 1024, 512, 512, 4096, 1024, 2048
+FLOPS = 2 * (2 * K * H * S + H * N * S)
+
+F32 = mybir.dt.float32
+BF16 = mybir.dt.bfloat16
+I32 = mybir.dt.int32
+U32 = mybir.dt.uint32
+U16 = mybir.dt.uint16
+U8 = mybir.dt.uint8
+FP8X4 = mybir.dt.float8_e4m3fn_x4
+FP4X4 = mybir.dt.float4_e2m1fn_x4
+ALU = mybir.AluOpType
+ACT = mybir.ActivationFunctionType
+
+P = 128
+PACK = 4
+PASSES = K // (P * PACK)
+HALF = S // 2
+HALVES = 2
+ROWTILES = N // P
+PAGES = 3
+MOVED = 112
+
+
+def tile_list_freight_match_listing_kernel(
+    tc, tab_words, tab_scales, offs, offs2, offs3, wa_words, wa_scales, wb, gain, wc, lane, wgo, out
+):
+    nc = tc.nc
+    with ExitStack() as ctx:
+        keep = ctx.enter_context(tc.tile_pool(name="keep", bufs=1))
+        ring = ctx.enter_context(tc.tile_pool(name="ring", bufs=3))
+        psum = ctx.enter_context(tc.psum_pool(name="psum", bufs=8))
+
+        def held(shape, dtype, name):
+            return keep.tile(shape, dtype, name=name, align_bytes=64)
+
+        list1 = held([P, S // 16], U16, "list1")
+        list2 = held([P, S // 16], U16, "list2")
+        list3 = held([P, S // 16], U16, "list3")
+        scale_window = held([P, T], U8, "scale_window")
+        word_window = [held([P, T], U32, f"word_window{a}") for a in range(PASSES)]
+        pages = [held([P, T2], F32, f"page{i}") for i in range(PAGES)]
+        wa_scale_raw = held([P, PASSES * H], U8, "wa_scale_raw")
+        ship_scales1 = held([P, S], U8, "ship_scales1")
+
+        nc.vector.memset(scale_window[:].bitcast(I32), 0)
+        nc.vector.memset(wa_scale_raw[:].bitcast(I32), 0)
+        nc.vector.memset(ship_scales1[:].bitcast(I32), 0)
+
+        words_hbm = [tab_words[a].rearrange("p t i -> p (t i)").bitcast(I32) for a in range(PASSES)]
+        nc.sync.dma_start(list1[:], offs)
+        nc.sync.dma_start(out=word_window[0][:, 0 : T // 2].bitcast(I32), in_=words_hbm[0][:, 0 : T // 2])
+        for q in range(4):
+            nc.sync.dma_start(
+                out=scale_window[32 * q : 32 * q + 8, :].bitcast(I32),
+                in_=tab_scales[:, 4 * q : 4 * q + 4, :].bitcast(I32),
+            )
+        nc.sync.dma_start(list2[:], offs2)
+        nc.sync.dma_start(out=word_window[0][:, T // 2 : T].bitcast(I32), in_=words_hbm[0][:, T // 2 : T])
+        for page in pages:
+            nc.vector.memset(page[:], 0.0)
+
+        wa_raw = held([P, PASSES, 2 * H], U8, "wa_raw")
+        for q in range(4):
+            nc.sync.dma_start(
+                out=wa_scale_raw[32 * q : 32 * q + 4, :].rearrange("r (a c) -> r a c", a=PASSES).bitcast(I32),
+                in_=wa_scales[:, 4 * q : 4 * q + 4, :].rearrange("a r c -> r a c").bitcast(I32),
+            )
+        nc.sync.dma_start(out=wa_raw[:].bitcast(I32), in_=wa_words.rearrange("a p c -> p a c").bitcast(I32))
+        wb_raw = [held([P, PACK, H], F32, f"wb_raw{a}") for a in range(PASSES)]
+        for a in range(PASSES):
+            nc.sync.dma_start(
+                out=wb_raw[a][:], in_=wb[512 * a : 512 * (a + 1), :].rearrange("(p j) c -> p j c", j=PACK)
+            )
+        nc.sync.dma_start(out=word_window[1][:].bitcast(I32), in_=words_hbm[1])
+        gain_col = held([P, PACK], F32, "gain_col")
+        nc.sync.dma_start(out=gain_col[:], in_=gain.rearrange("(p t) -> p t", t=PACK))
+        wc_raw = held([P, PACK, N], F32, "wc_raw")
+        nc.sync.dma_start(out=wc_raw[:], in_=wc.rearrange("(p j) c -> p j c", j=PACK))
+        nc.sync.dma_start(list3[:], offs3)
+        wgo_sb = held([P, S], F32, "wgo_sb")
+        lane_sb = [held([P, S], F32, f"lane{n}") for n in range(ROWTILES)]
+        nc.sync.dma_start(out=lane_sb[0][:], in_=lane[0:P, :])
+        nc.sync.dma_start(out=wgo_sb[:], in_=wgo)
+        for n in range(1, ROWTILES):
+            nc.sync.dma_start(out=lane_sb[n][:], in_=lane[n * P : (n + 1) * P, :])
+
+        wa_dealt = held([P, PASSES * 2 * H], U8, "wa_dealt")
+        nc.scalar.copy(
+            out=wa_dealt[:].bitcast(U16).rearrange("p (a t m) -> p a m t", a=PASSES, t=PACK),
+            in_=wa_raw[:].bitcast(U16).rearrange("p a (m t) -> p a m t", t=PACK),
+        )
+        wa_scale = held([P, PASSES * H], U8, "wa_scale")
+        nc.vector.tensor_copy(
+            out=wa_scale[:].rearrange("p (a t m) -> p a m t", a=PASSES, t=PACK),
+            in_=wa_scale_raw[:].rearrange("p (a m t) -> p a m t", a=PASSES, t=PACK),
+        )
+
+        ship_scales0 = held([P, S], U8, "ship_scales0")
+        truck_scales = held([P, S], U8, "truck_scales")
+        nc.vector.tensor_copy(ship_scales0[:], scale_window[:].indirect(list1[:]))
+        nc.scalar.dma_start(out=ship_scales1[0:MOVED, :].bitcast(I32), in_=ship_scales0[4 : 4 + MOVED, :].bitcast(I32))
+        nc.vector.tensor_copy(truck_scales[:], scale_window[:].indirect(list2[:]))
+        ship_words0 = held([P, S], U32, "ship_words0")
+        ship_words1 = [held([P, HALF], U32, f"ship_words1_{h}") for h in range(HALVES)]
+        truck_words0 = held([P, S], U32, "truck_words0")
+        truck_words1 = [held([P, HALF], U32, f"truck_words1_{h}") for h in range(HALVES)]
+        nc.vector.tensor_copy(ship_words0[:], word_window[0][:].indirect(list1[:]))
+        nc.vector.tensor_copy(truck_words0[:], word_window[0][:].indirect(list2[:]))
+
+        def gather_pass1(h):
+            nc.vector.tensor_copy(ship_words1[h][:], word_window[1][:].indirect(list1[:, 32 * h : 32 * (h + 1)]))
+            nc.vector.tensor_copy(truck_words1[h][:], word_window[1][:].indirect(list2[:, 32 * h : 32 * (h + 1)]))
+
+        def quantise(grouped, width, name):
+            codes = held([P, width], U32, name + "_codes")
+            scales = held([P, width], U8, name + "_scales")
+            nc.vector.quantize_mx(out=codes[:].bitcast(FP8X4), scales=scales[:], in_=grouped[:])
+            return codes, scales
+
+        def round_wb(a):
+            grouped = held([P, PACK * H], BF16, f"wb_grouped{a}")
+            nc.scalar.copy(
+                out=grouped[:].rearrange("p (t m j) -> p m j t", t=PACK, j=PACK),
+                in_=wb_raw[a][:].rearrange("p j (m t) -> p m j t", t=PACK),
+            )
+            return grouped
+
+        ship_planes = [ship_scales0, ship_scales1]
+        ship = {}
+        truck = {}
+
+        def ship_half(h):
+            cols = slice(h * HALF, (h + 1) * HALF)
+            moving = [ship_words0[:, cols], ship_words1[h][:]]
+            for t in range(PACK):
+                acc = psum.tile([P, HALF], F32, name="acc")
+                for a in range(PASSES):
+                    c0 = a * H + t * P
+                    nc.tensor.matmul_mx(
+                        out=acc[:],
+                        lhsT=wa_dealt[:, 2 * c0 : 2 * (c0 + P)].bitcast(FP4X4),
+                        lhsT_scale=wa_scale[:, c0 : c0 + P],
+                        rhs=moving[a].bitcast(FP8X4),
+                        rhs_scale=ship_planes[a][:, cols],
+                        start=(a == 0),
+                        stop=(a == PASSES - 1),
+                    )
+                ship[h, t] = held([P, HALF], F32, f"ship{h}_{t}")
+                nc.scalar.activation(out=ship[h, t][:], in_=acc[:], func=ACT.Tanh)
+
+        def truck_half(h, wb_q):
+            cols = slice(h * HALF, (h + 1) * HALF)
+            moving = [truck_words0[:, cols], truck_words1[h][:]]
+            for t in range(PACK):
+                acc = psum.tile([P, HALF], F32, name="acc")
+                for a in range(PASSES):
+                    nc.tensor.matmul_mx(
+                        out=acc[:],
+                        lhsT=wb_q[a][0][:, t * P : (t + 1) * P].bitcast(FP8X4),
+                        lhsT_scale=wb_q[a][1][:, t * P : (t + 1) * P],
+                        rhs=moving[a].bitcast(FP8X4),
+                        rhs_scale=truck_scales[4 * a : P, cols],
+                        start=(a == 0),
+                        stop=(a == PASSES - 1),
+                    )
+                truck[h, t] = held([P, HALF], F32, f"truck{h}_{t}")
+                nc.scalar.activation(out=truck[h, t][:], in_=acc[:], func=ACT.Sin)
+
+        def smaller(h):
+            for t in range(PACK):
+                nc.vector.tensor_tensor(ship[h, t][:], ship[h, t][:], truck[h, t][:], ALU.min)
+
+        def make_z(h, on_vector):
+            planar = held([P, PACK, HALF], BF16, f"z_planar{h}")
+            grouped = held([P, PACK * HALF], BF16, f"z_grouped{h}")
+            for t in range(PACK):
+                if on_vector:
+                    nc.vector.tensor_scalar(planar[:, t, :], ship[h, t][:], gain_col[:, t : t + 1], None, ALU.mult)
+                else:
+                    nc.scalar.activation(
+                        out=planar[:, t, :], in_=ship[h, t][:], func=ACT.Copy, scale=gain_col[:, t : t + 1]
+                    )
+            dst = grouped[:].rearrange("p (c i t) -> p c t i", i=4, t=PACK)
+            src = planar[:].rearrange("p t (c i) -> p c t i", i=4)
+            if on_vector:
+                nc.vector.tensor_copy(out=dst, in_=src)
+            else:
+                nc.scalar.copy(out=dst, in_=src)
+            return grouped
+
+        wb_q = [quantise(round_wb(a), H, f"wb{a}") for a in range(PASSES)]
+        for h in range(HALVES):
+            gather_pass1(h)
+        ship_half(0)
+        truck_half(0, wb_q)
+        wc_grouped = held([P, PACK * N], BF16, "wc_grouped")
+        nc.scalar.copy(
+            out=wc_grouped[:].rearrange("p (c i j) -> p c j i", i=4, j=PACK),
+            in_=wc_raw[:].rearrange("p j (c i) -> p c j i", i=4),
+        )
+        truck_half(1, wb_q)
+        ship_half(1)
+        smaller(0)
+        z0 = make_z(0, True)
+        wc_codes, wc_scales = quantise(wc_grouped, N, "wc")
+        z_q = {0: quantise(z0, HALF, "z0")}
+        smaller(1)
+        z1 = make_z(1, False)
+
+        def listing(n, h):
+            cols = slice(h * HALF, (h + 1) * HALF)
+            acc = psum.tile([P, HALF], F32, name="acc")
+            nc.tensor.matmul_mx(
+                out=acc[:],
+                lhsT=wc_codes[:, n * P : (n + 1) * P].bitcast(FP8X4),
+                lhsT_scale=wc_scales[:, n * P : (n + 1) * P],
+                rhs=z_q[h][0][:].bitcast(FP8X4),
+                rhs_scale=z_q[h][1][:],
+                start=True,
+                stop=True,
+            )
+            y = ring.tile([P, HALF], F32, name="y")
+            nc.vector.tensor_tensor(y[:], acc[:], lane_sb[n][:, cols], ALU.mult)
+            return y
+
+        def place(n, h, y):
+            cols = slice(h * HALF, (h + 1) * HALF)
+            page = pages[n % PAGES]
+            nc.vector.tensor_tensor(
+                page[:].indirect(list3[:, 32 * h : 32 * (h + 1)]), y[:], wgo_sb[:, cols], ALU.mult
+            )
+            if (n, h) in last_of_page:
+                nc.sync.dma_start(out=out[n * P : (n + 1) * P, :], in_=page[:])
+
+        steps = [(0, 0), (1, 0), (2, 0), (0, 1), (1, 1), (3, 0), (2, 1), (3, 1)]
+        last_of_page = {(n, 1) for n in range(ROWTILES)}
+        ahead = listing(*steps[0])
+        for i, (n, h) in enumerate(steps):
+            y = ahead
+            if i + 1 < len(steps):
+                if steps[i + 1] == (0, 1):
+                    z_q[1] = quantise(z1, HALF, "z1")
+                ahead = listing(*steps[i + 1])
+            place(n, h, y)

@@ -35,15 +35,14 @@ def tile_list_freight_match_listing_kernel(
         ring = ctx.enter_context(tc.tile_pool(name="ring", bufs=3))
         psum = ctx.enter_context(tc.psum_pool(name="psum", bufs=8))
 
-        def held(shape, dtype, name):
-            return keep.tile(shape, dtype, name=name, align_bytes=64)
+        def held(shape, dtype, name, tag=None):
+            return keep.tile(shape, dtype, name=name, tag=tag or name, align_bytes=64)
 
         list1 = held([P, S // 16], U16, "list1")
         list2 = held([P, S // 16], U16, "list2")
         list3 = held([P, S // 16], U16, "list3")
         scale_window = held([P, T], U8, "scale_window")
         word_window = [held([P, T], U32, f"word_window{a}") for a in range(PASSES)]
-        pages = [held([P, T2], F32, f"page{i}") for i in range(PAGES)]
         wa_scale_raw = held([P, PASSES * H], U8, "wa_scale_raw")
         ship_scales1 = held([P, S], U8, "ship_scales1")
 
@@ -61,9 +60,6 @@ def tile_list_freight_match_listing_kernel(
             )
         nc.sync.dma_start(list2[:], offs2)
         nc.sync.dma_start(out=word_window[0][:, T // 2 : T].bitcast(I32), in_=words_hbm[0][:, T // 2 : T])
-        for page in pages:
-            nc.vector.memset(page[:], 0.0)
-
         wa_raw = held([P, PASSES, 2 * H], U8, "wa_raw")
         for q in range(4):
             nc.sync.dma_start(
@@ -91,13 +87,13 @@ def tile_list_freight_match_listing_kernel(
 
         wa_dealt = held([P, PASSES * 2 * H], U8, "wa_dealt")
         nc.scalar.copy(
-            out=wa_dealt[:].bitcast(U16).rearrange("p (a t m) -> p a m t", a=PASSES, t=PACK),
-            in_=wa_raw[:].bitcast(U16).rearrange("p a (m t) -> p a m t", t=PACK),
+            out=wa_dealt[:].bitcast(U16).rearrange("p (a t m) -> p a t m", a=PASSES, t=PACK),
+            in_=wa_raw[:].bitcast(U16).rearrange("p a (m t) -> p a t m", t=PACK),
         )
         wa_scale = held([P, PASSES * H], U8, "wa_scale")
         nc.vector.tensor_copy(
-            out=wa_scale[:].rearrange("p (a t m) -> p a m t", a=PASSES, t=PACK),
-            in_=wa_scale_raw[:].rearrange("p (a m t) -> p a m t", a=PASSES, t=PACK),
+            out=wa_scale[:].rearrange("p (a t m) -> p a t m", a=PASSES, t=PACK),
+            in_=wa_scale_raw[:].rearrange("p (a m t) -> p a t m", a=PASSES, t=PACK),
         )
 
         ship_scales0 = held([P, S], U8, "ship_scales0")
@@ -106,15 +102,19 @@ def tile_list_freight_match_listing_kernel(
         nc.scalar.dma_start(out=ship_scales1[0:MOVED, :].bitcast(I32), in_=ship_scales0[4 : 4 + MOVED, :].bitcast(I32))
         nc.vector.tensor_copy(truck_scales[:], scale_window[:].indirect(list2[:]))
         ship_words0 = held([P, S], U32, "ship_words0")
-        ship_words1 = [held([P, HALF], U32, f"ship_words1_{h}") for h in range(HALVES)]
         truck_words0 = held([P, S], U32, "truck_words0")
-        truck_words1 = [held([P, HALF], U32, f"truck_words1_{h}") for h in range(HALVES)]
         nc.vector.tensor_copy(ship_words0[:], word_window[0][:].indirect(list1[:]))
         nc.vector.tensor_copy(truck_words0[:], word_window[0][:].indirect(list2[:]))
 
+        ship_words1 = []
+        truck_words1 = []
+
         def gather_pass1(h):
-            nc.vector.tensor_copy(ship_words1[h][:], word_window[1][:].indirect(list1[:, 32 * h : 32 * (h + 1)]))
-            nc.vector.tensor_copy(truck_words1[h][:], word_window[1][:].indirect(list2[:, 32 * h : 32 * (h + 1)]))
+            both = held([P, 2 * HALF], U32, f"words1_{h}")
+            ship_words1.append(both[:, 0:HALF])
+            truck_words1.append(both[:, HALF : 2 * HALF])
+            nc.vector.tensor_copy(ship_words1[h], word_window[1][:].indirect(list1[:, 32 * h : 32 * (h + 1)]))
+            nc.vector.tensor_copy(truck_words1[h], word_window[1][:].indirect(list2[:, 32 * h : 32 * (h + 1)]))
 
         def quantise(grouped, width, name):
             codes = held([P, width], U32, name + "_codes")
@@ -125,8 +125,8 @@ def tile_list_freight_match_listing_kernel(
         def round_wb(a):
             grouped = held([P, PACK * H], BF16, f"wb_grouped{a}")
             nc.scalar.copy(
-                out=grouped[:].rearrange("p (t m j) -> p m j t", t=PACK, j=PACK),
-                in_=wb_raw[a][:].rearrange("p j (m t) -> p m j t", t=PACK),
+                out=grouped[:].rearrange("p (t m j) -> p m t j", t=PACK, j=PACK),
+                in_=wb_raw[a][:].rearrange("p j (m t) -> p m t j", t=PACK),
             )
             return grouped
 
@@ -136,7 +136,7 @@ def tile_list_freight_match_listing_kernel(
 
         def ship_half(h):
             cols = slice(h * HALF, (h + 1) * HALF)
-            moving = [ship_words0[:, cols], ship_words1[h][:]]
+            moving = [ship_words0[:, cols], ship_words1[h]]
             for t in range(PACK):
                 acc = psum.tile([P, HALF], F32, name="acc")
                 for a in range(PASSES):
@@ -155,7 +155,7 @@ def tile_list_freight_match_listing_kernel(
 
         def truck_half(h, wb_q):
             cols = slice(h * HALF, (h + 1) * HALF)
-            moving = [truck_words0[:, cols], truck_words1[h][:]]
+            moving = [truck_words0[:, cols], truck_words1[h]]
             for t in range(PACK):
                 acc = psum.tile([P, HALF], F32, name="acc")
                 for a in range(PASSES):
@@ -171,20 +171,26 @@ def tile_list_freight_match_listing_kernel(
                 truck[h, t] = held([P, HALF], F32, f"truck{h}_{t}")
                 nc.scalar.activation(out=truck[h, t][:], in_=acc[:], func=ACT.Sin)
 
-        def smaller(h):
-            for t in range(PACK):
-                nc.vector.tensor_tensor(ship[h, t][:], ship[h, t][:], truck[h, t][:], ALU.min)
-
         def make_z(h, on_vector):
             planar = held([P, PACK, HALF], BF16, f"z_planar{h}")
             grouped = held([P, PACK * HALF], BF16, f"z_grouped{h}")
-            for t in range(PACK):
+
+            def smaller(t):
+                nc.vector.tensor_tensor(ship[h, t][:], ship[h, t][:], truck[h, t][:], ALU.min)
+
+            def gained(t):
                 if on_vector:
                     nc.vector.tensor_scalar(planar[:, t, :], ship[h, t][:], gain_col[:, t : t + 1], None, ALU.mult)
                 else:
                     nc.scalar.activation(
                         out=planar[:, t, :], in_=ship[h, t][:], func=ACT.Copy, scale=gain_col[:, t : t + 1]
                     )
+
+            smaller(0)
+            for t in range(1, PACK):
+                smaller(t)
+                gained(t - 1)
+            gained(PACK - 1)
             dst = grouped[:].rearrange("p (c i t) -> p c t i", i=4, t=PACK)
             src = planar[:].rearrange("p t (c i) -> p c t i", i=4)
             if on_vector:
@@ -194,6 +200,11 @@ def tile_list_freight_match_listing_kernel(
             return grouped
 
         wb_q = [quantise(round_wb(a), H, f"wb{a}") for a in range(PASSES)]
+        pages = []
+        for i, tag in enumerate(["wa_raw", "wa_scale_raw", "wb_raw0"]):
+            pages.append(held([P, T2], F32, f"page{i}", tag))
+            for c in range(0, T2, HALF):
+                nc.gpsimd.memset(pages[i][:, c : c + HALF], 0.0)
         for h in range(HALVES):
             gather_pass1(h)
         ship_half(0)
@@ -205,11 +216,9 @@ def tile_list_freight_match_listing_kernel(
         )
         truck_half(1, wb_q)
         ship_half(1)
-        smaller(0)
         z0 = make_z(0, True)
         wc_codes, wc_scales = quantise(wc_grouped, N, "wc")
         z_q = {0: quantise(z0, HALF, "z0")}
-        smaller(1)
         z1 = make_z(1, False)
 
         def listing(n, h):

@@ -24,6 +24,7 @@ HALVES = 2
 ROWTILES = N // P
 PAGES = 3
 MOVED = 112
+FIRST = 1024
 
 
 def tile_list_freight_match_listing_kernel(
@@ -43,23 +44,26 @@ def tile_list_freight_match_listing_kernel(
         list3 = held([P, S // 16], U16, "list3")
         scale_window = held([P, T], U8, "scale_window")
         word_window = [held([P, T], U32, f"word_window{a}") for a in range(PASSES)]
+        pages = [held([P, T2], F32, f"page{i}") for i in range(PAGES)]
         wa_scale_raw = held([P, PASSES * H], U8, "wa_scale_raw")
         ship_scales1 = held([P, S], U8, "ship_scales1")
+        truck_scales1 = held([P, S], U8, "truck_scales1")
 
         nc.vector.memset(scale_window[:].bitcast(I32), 0)
         nc.vector.memset(wa_scale_raw[:].bitcast(I32), 0)
-        nc.vector.memset(ship_scales1[:].bitcast(I32), 0)
+        nc.vector.memset(ship_scales1[96:P, :].bitcast(I32), 0)
+        nc.vector.memset(truck_scales1[96:P, :].bitcast(I32), 0)
 
         words_hbm = [tab_words[a].rearrange("p t i -> p (t i)").bitcast(I32) for a in range(PASSES)]
         nc.sync.dma_start(list1[:], offs)
-        nc.sync.dma_start(out=word_window[0][:, 0 : T // 2].bitcast(I32), in_=words_hbm[0][:, 0 : T // 2])
-        for q in range(4):
-            nc.sync.dma_start(
-                out=scale_window[32 * q : 32 * q + 8, :].bitcast(I32),
-                in_=tab_scales[:, 4 * q : 4 * q + 4, :].bitcast(I32),
-            )
+        nc.sync.dma_start(out=word_window[0][:, 0 : FIRST].bitcast(I32), in_=words_hbm[0][:, 0 : FIRST])
+        scale_rows = tab_scales.rearrange("a (q r) t -> r q a t", r=4)
+        for r in range(4):
+            nc.sync.dma_start(out=scale_window[r:P:16, :].bitcast(I32), in_=scale_rows[r].bitcast(I32))
         nc.sync.dma_start(list2[:], offs2)
-        nc.sync.dma_start(out=word_window[0][:, T // 2 : T].bitcast(I32), in_=words_hbm[0][:, T // 2 : T])
+        nc.sync.dma_start(out=word_window[0][:, FIRST : T].bitcast(I32), in_=words_hbm[0][:, FIRST : T])
+        for page in pages:
+            nc.vector.memset(page[:], 0.0)
         wa_raw = held([P, PASSES, 2 * H], U8, "wa_raw")
         for q in range(4):
             nc.sync.dma_start(
@@ -73,6 +77,19 @@ def tile_list_freight_match_listing_kernel(
                 out=wb_raw[a][:], in_=wb[512 * a : 512 * (a + 1), :].rearrange("(p j) c -> p j c", j=PACK)
             )
         nc.sync.dma_start(out=word_window[1][:].bitcast(I32), in_=words_hbm[1])
+
+        wa_dealt = held([P, PASSES * 2 * H], U8, "wa_dealt")
+        nc.scalar.copy(
+            out=wa_dealt[:].bitcast(U16).rearrange("p (a t m) -> p a t m", a=PASSES, t=PACK),
+            in_=wa_raw[:].bitcast(U16).rearrange("p a (m t) -> p a t m", t=PACK),
+        )
+
+        ship_scales0 = held([P, S], U8, "ship_scales0")
+        truck_scales = held([P, S], U8, "truck_scales")
+        nc.vector.tensor_copy(ship_scales0[:], scale_window[:].indirect(list1[:]))
+        nc.vector.tensor_copy(truck_scales[:], scale_window[:].indirect(list2[:]))
+        nc.sync.dma_start(out=ship_scales1[0:MOVED, :].bitcast(I32), in_=ship_scales0[16:P, :].bitcast(I32))
+        nc.sync.dma_start(out=truck_scales1[0:MOVED, :].bitcast(I32), in_=truck_scales[16:P, :].bitcast(I32))
         gain_col = held([P, PACK], F32, "gain_col")
         nc.sync.dma_start(out=gain_col[:], in_=gain.rearrange("(p t) -> p t", t=PACK))
         wc_raw = held([P, PACK, N], F32, "wc_raw")
@@ -85,26 +102,16 @@ def tile_list_freight_match_listing_kernel(
         for n in range(1, ROWTILES):
             nc.sync.dma_start(out=lane_sb[n][:], in_=lane[n * P : (n + 1) * P, :])
 
-        wa_dealt = held([P, PASSES * 2 * H], U8, "wa_dealt")
-        nc.scalar.copy(
-            out=wa_dealt[:].bitcast(U16).rearrange("p (a t m) -> p a t m", a=PASSES, t=PACK),
-            in_=wa_raw[:].bitcast(U16).rearrange("p a (m t) -> p a t m", t=PACK),
-        )
+        ship_words0 = held([P, S], U32, "ship_words0")
+        truck_words0 = held([P, S], U32, "truck_words0")
+        nc.vector.tensor_copy(ship_words0[:], word_window[0][:].indirect(list1[:]))
+        nc.vector.tensor_copy(truck_words0[:], word_window[0][:].indirect(list2[:]))
+
         wa_scale = held([P, PASSES * H], U8, "wa_scale")
         nc.vector.tensor_copy(
             out=wa_scale[:].rearrange("p (a t m) -> p a t m", a=PASSES, t=PACK),
             in_=wa_scale_raw[:].rearrange("p (a m t) -> p a t m", a=PASSES, t=PACK),
         )
-
-        ship_scales0 = held([P, S], U8, "ship_scales0")
-        truck_scales = held([P, S], U8, "truck_scales")
-        nc.vector.tensor_copy(ship_scales0[:], scale_window[:].indirect(list1[:]))
-        nc.scalar.dma_start(out=ship_scales1[0:MOVED, :].bitcast(I32), in_=ship_scales0[4 : 4 + MOVED, :].bitcast(I32))
-        nc.vector.tensor_copy(truck_scales[:], scale_window[:].indirect(list2[:]))
-        ship_words0 = held([P, S], U32, "ship_words0")
-        truck_words0 = held([P, S], U32, "truck_words0")
-        nc.vector.tensor_copy(ship_words0[:], word_window[0][:].indirect(list1[:]))
-        nc.vector.tensor_copy(truck_words0[:], word_window[0][:].indirect(list2[:]))
 
         ship_words1 = []
         truck_words1 = []
@@ -164,7 +171,7 @@ def tile_list_freight_match_listing_kernel(
                         lhsT=wb_q[a][0][:, t * P : (t + 1) * P].bitcast(FP8X4),
                         lhsT_scale=wb_q[a][1][:, t * P : (t + 1) * P],
                         rhs=moving[a].bitcast(FP8X4),
-                        rhs_scale=truck_scales[4 * a : P, cols],
+                        rhs_scale=[truck_scales, truck_scales1][a][:, cols],
                         start=(a == 0),
                         stop=(a == PASSES - 1),
                     )
@@ -200,11 +207,6 @@ def tile_list_freight_match_listing_kernel(
             return grouped
 
         wb_q = [quantise(round_wb(a), H, f"wb{a}") for a in range(PASSES)]
-        pages = []
-        for i, tag in enumerate(["wa_raw", "wa_scale_raw", "wb_raw0"]):
-            pages.append(held([P, T2], F32, f"page{i}", tag))
-            for c in range(0, T2, HALF):
-                nc.gpsimd.memset(pages[i][:, c : c + HALF], 0.0)
         for h in range(HALVES):
             gather_pass1(h)
         ship_half(0)

@@ -63,7 +63,7 @@ def tile_list_freight_match_listing_kernel(
         nc.sync.dma_start(list2[:], offs2)
         nc.sync.dma_start(out=word_window[0][:, FIRST : T].bitcast(I32), in_=words_hbm[0][:, FIRST : T])
         for page in pages:
-            nc.vector.memset(page[:], 0.0)
+            nc.vector.memset(page[:].bitcast(I32), 0)
         wa_raw = held([P, PASSES, 2 * H], U8, "wa_raw")
         for q in range(4):
             nc.sync.dma_start(
@@ -92,15 +92,7 @@ def tile_list_freight_match_listing_kernel(
         nc.sync.dma_start(out=truck_scales1[0:MOVED, :].bitcast(I32), in_=truck_scales[16:P, :].bitcast(I32))
         gain_col = held([P, PACK], F32, "gain_col")
         nc.sync.dma_start(out=gain_col[:], in_=gain.rearrange("(p t) -> p t", t=PACK))
-        wc_raw = held([P, PACK, N], F32, "wc_raw")
-        nc.sync.dma_start(out=wc_raw[:], in_=wc.rearrange("(p j) c -> p j c", j=PACK))
         nc.sync.dma_start(list3[:], offs3)
-        wgo_sb = held([P, S], F32, "wgo_sb")
-        lane_sb = [held([P, S], F32, f"lane{n}") for n in range(ROWTILES)]
-        nc.sync.dma_start(out=lane_sb[0][:], in_=lane[0:P, :])
-        nc.sync.dma_start(out=wgo_sb[:], in_=wgo)
-        for n in range(1, ROWTILES):
-            nc.sync.dma_start(out=lane_sb[n][:], in_=lane[n * P : (n + 1) * P, :])
 
         ship_words0 = held([P, S], U32, "ship_words0")
         truck_words0 = held([P, S], U32, "truck_words0")
@@ -207,6 +199,14 @@ def tile_list_freight_match_listing_kernel(
             return grouped
 
         wb_q = [quantise(round_wb(a), H, f"wb{a}") for a in range(PASSES)]
+        wc_raw = held([P, PACK, N], F32, "wc_raw", "wb_raw0")
+        nc.sync.dma_start(out=wc_raw[:], in_=wc.rearrange("(p j) c -> p j c", j=PACK))
+        wgo_sb = held([P, S], F32, "wgo_sb", "wb_grouped0")
+        nc.sync.dma_start(out=wgo_sb[:], in_=wgo)
+        lane_sb = []
+        for n, tag in enumerate(["scale_window", "word_window0", "wb_raw1", "wb_grouped1"]):
+            lane_sb.append(held([P, S], F32, f"lane{n}", tag))
+            nc.sync.dma_start(out=lane_sb[n][:], in_=lane[n * P : (n + 1) * P, :])
         for h in range(HALVES):
             gather_pass1(h)
         ship_half(0)

@@ -19,12 +19,14 @@ ACT = mybir.ActivationFunctionType
 P = 128
 PACK = 4
 PASSES = K // (P * PACK)
+QUADRANTS = 4
 HALF = S // 2
-HALVES = 2
-ROWTILES = N // P
+HALF_LIST = HALF // 16
+ROW_TILES = N // P
 PAGES = 3
-MOVED = 112
-FIRST = 1024
+PASS_SHIFT = 16
+FIRST_WORDS = 1024
+RUN = 4
 
 
 def tile_list_freight_match_listing_kernel(
@@ -36,15 +38,22 @@ def tile_list_freight_match_listing_kernel(
         ring = ctx.enter_context(tc.tile_pool(name="ring", bufs=3))
         psum = ctx.enter_context(tc.psum_pool(name="psum", bufs=8))
 
-        def held(shape, dtype, name, tag=None):
-            return keep.tile(shape, dtype, name=name, tag=tag or name, align_bytes=64)
+        def held(shape, dtype, name, reuse=None):
+            return keep.tile(shape, dtype, name=name, tag=reuse or name, align_bytes=64)
+
+        def half_of(list_tile, h):
+            return list_tile[:, HALF_LIST * h : HALF_LIST * (h + 1)]
+
+        def cleared_page(i, reuse=None):
+            page = held([P, T2], F32, f"page{i}", reuse)
+            nc.vector.memset(page[:].bitcast(I32), 0)
+            return page
 
         list1 = held([P, S // 16], U16, "list1")
         list2 = held([P, S // 16], U16, "list2")
         list3 = held([P, S // 16], U16, "list3")
         scale_window = held([P, T], U8, "scale_window")
         word_window = [held([P, T], U32, f"word_window{a}") for a in range(PASSES)]
-        pages = [held([P, T2], F32, f"page{i}") for i in range(PAGES)]
         wa_scale_raw = held([P, PASSES * H], U8, "wa_scale_raw")
         ship_scales1 = held([P, S], U8, "ship_scales1")
         truck_scales1 = held([P, S], U8, "truck_scales1")
@@ -56,26 +65,25 @@ def tile_list_freight_match_listing_kernel(
 
         words_hbm = [tab_words[a].rearrange("p t i -> p (t i)").bitcast(I32) for a in range(PASSES)]
         nc.sync.dma_start(list1[:], offs)
-        nc.sync.dma_start(out=word_window[0][:, 0 : FIRST].bitcast(I32), in_=words_hbm[0][:, 0 : FIRST])
+        nc.sync.dma_start(out=word_window[0][:, 0:FIRST_WORDS].bitcast(I32), in_=words_hbm[0][:, 0:FIRST_WORDS])
         scale_rows = tab_scales.rearrange("a (q r) t -> r q a t", r=4)
         for r in range(4):
-            nc.sync.dma_start(out=scale_window[r:P:16, :].bitcast(I32), in_=scale_rows[r].bitcast(I32))
+            nc.sync.dma_start(out=scale_window[r:P:PASS_SHIFT, :].bitcast(I32), in_=scale_rows[r].bitcast(I32))
         nc.sync.dma_start(list2[:], offs2)
-        nc.sync.dma_start(out=word_window[0][:, FIRST : T].bitcast(I32), in_=words_hbm[0][:, FIRST : T])
-        for page in pages:
-            nc.vector.memset(page[:].bitcast(I32), 0)
+        nc.sync.dma_start(out=word_window[0][:, FIRST_WORDS:T].bitcast(I32), in_=words_hbm[0][:, FIRST_WORDS:T])
+
+        pages = {i: cleared_page(i) for i in range(PAGES - 1)}
+
         wa_raw = held([P, PASSES, 2 * H], U8, "wa_raw")
-        for q in range(4):
+        for q in range(QUADRANTS):
             nc.sync.dma_start(
                 out=wa_scale_raw[32 * q : 32 * q + 4, :].rearrange("r (a c) -> r a c", a=PASSES).bitcast(I32),
                 in_=wa_scales[:, 4 * q : 4 * q + 4, :].rearrange("a r c -> r a c").bitcast(I32),
             )
         nc.sync.dma_start(out=wa_raw[:].bitcast(I32), in_=wa_words.rearrange("a p c -> p a c").bitcast(I32))
         wb_raw = [held([P, PACK, H], F32, f"wb_raw{a}") for a in range(PASSES)]
-        for a in range(PASSES):
-            nc.sync.dma_start(
-                out=wb_raw[a][:], in_=wb[512 * a : 512 * (a + 1), :].rearrange("(p j) c -> p j c", j=PACK)
-            )
+        wb_rows = wb.rearrange("(a p j) c -> a p j c", a=PASSES, j=PACK)
+        nc.sync.dma_start(out=wb_raw[0][:], in_=wb_rows[0])
         nc.sync.dma_start(out=word_window[1][:].bitcast(I32), in_=words_hbm[1])
 
         wa_dealt = held([P, PASSES * 2 * H], U8, "wa_dealt")
@@ -85,11 +93,17 @@ def tile_list_freight_match_listing_kernel(
         )
 
         ship_scales0 = held([P, S], U8, "ship_scales0")
-        truck_scales = held([P, S], U8, "truck_scales")
+        truck_scales0 = held([P, S], U8, "truck_scales0")
         nc.vector.tensor_copy(ship_scales0[:], scale_window[:].indirect(list1[:]))
-        nc.vector.tensor_copy(truck_scales[:], scale_window[:].indirect(list2[:]))
-        nc.sync.dma_start(out=ship_scales1[0:MOVED, :].bitcast(I32), in_=ship_scales0[16:P, :].bitcast(I32))
-        nc.sync.dma_start(out=truck_scales1[0:MOVED, :].bitcast(I32), in_=truck_scales[16:P, :].bitcast(I32))
+        nc.vector.tensor_copy(truck_scales0[:], scale_window[:].indirect(list2[:]))
+        for both_passes, pass1 in ((ship_scales0, ship_scales1), (truck_scales0, truck_scales1)):
+            nc.sync.dma_start(
+                out=pass1[0 : P - PASS_SHIFT, :].bitcast(I32), in_=both_passes[PASS_SHIFT:P, :].bitcast(I32)
+            )
+        ship_scales = [ship_scales0, ship_scales1]
+        truck_scales = [truck_scales0, truck_scales1]
+
+        nc.sync.dma_start(out=wb_raw[1][:], in_=wb_rows[1])
         gain_col = held([P, PACK], F32, "gain_col")
         nc.sync.dma_start(out=gain_col[:], in_=gain.rearrange("(p t) -> p t", t=PACK))
         nc.sync.dma_start(list3[:], offs3)
@@ -108,12 +122,12 @@ def tile_list_freight_match_listing_kernel(
         ship_words1 = []
         truck_words1 = []
 
-        def gather_pass1(h):
-            both = held([P, 2 * HALF], U32, f"words1_{h}")
-            ship_words1.append(both[:, 0:HALF])
-            truck_words1.append(both[:, HALF : 2 * HALF])
-            nc.vector.tensor_copy(ship_words1[h], word_window[1][:].indirect(list1[:, 32 * h : 32 * (h + 1)]))
-            nc.vector.tensor_copy(truck_words1[h], word_window[1][:].indirect(list2[:, 32 * h : 32 * (h + 1)]))
+        def gather_pass1(h, reuse=None):
+            both_lists = held([P, 2 * HALF], U32, f"words1_{h}", reuse)
+            ship_words1.append(both_lists[:, 0:HALF])
+            truck_words1.append(both_lists[:, HALF : 2 * HALF])
+            nc.vector.tensor_copy(ship_words1[h], word_window[1][:].indirect(half_of(list1, h)))
+            nc.vector.tensor_copy(truck_words1[h], word_window[1][:].indirect(half_of(list2, h)))
 
         def quantise(grouped, width, name):
             codes = held([P, width], U32, name + "_codes")
@@ -121,15 +135,20 @@ def tile_list_freight_match_listing_kernel(
             nc.vector.quantize_mx(out=codes[:].bitcast(FP8X4), scales=scales[:], in_=grouped[:])
             return codes, scales
 
-        def round_wb(a):
+        def round_wb(a, copy):
             grouped = held([P, PACK * H], BF16, f"wb_grouped{a}")
-            nc.scalar.copy(
+            copy(
                 out=grouped[:].rearrange("p (t m j) -> p m t j", t=PACK, j=PACK),
                 in_=wb_raw[a][:].rearrange("p j (m t) -> p m t j", t=PACK),
             )
             return grouped
 
-        ship_planes = [ship_scales0, ship_scales1]
+        def interleave(copy, grouped, planar):
+            copy(
+                out=grouped[:].rearrange("p (c i j) -> p c j i", i=RUN, j=PACK),
+                in_=planar[:].rearrange("p j (c i) -> p c j i", i=RUN),
+            )
+
         ship = {}
         truck = {}
 
@@ -145,32 +164,39 @@ def tile_list_freight_match_listing_kernel(
                         lhsT=wa_dealt[:, 2 * c0 : 2 * (c0 + P)].bitcast(FP4X4),
                         lhsT_scale=wa_scale[:, c0 : c0 + P],
                         rhs=moving[a].bitcast(FP8X4),
-                        rhs_scale=ship_planes[a][:, cols],
+                        rhs_scale=ship_scales[a][:, cols],
                         start=(a == 0),
                         stop=(a == PASSES - 1),
                     )
                 ship[h, t] = held([P, HALF], F32, f"ship{h}_{t}")
                 nc.scalar.activation(out=ship[h, t][:], in_=acc[:], func=ACT.Tanh)
 
-        def truck_half(h, wb_q):
+        def truck_half(h):
             cols = slice(h * HALF, (h + 1) * HALF)
             moving = [truck_words0[:, cols], truck_words1[h]]
             for t in range(PACK):
                 acc = psum.tile([P, HALF], F32, name="acc")
                 for a in range(PASSES):
+                    wb_codes, wb_scales = wb_q[a]
                     nc.tensor.matmul_mx(
                         out=acc[:],
-                        lhsT=wb_q[a][0][:, t * P : (t + 1) * P].bitcast(FP8X4),
-                        lhsT_scale=wb_q[a][1][:, t * P : (t + 1) * P],
+                        lhsT=wb_codes[:, t * P : (t + 1) * P].bitcast(FP8X4),
+                        lhsT_scale=wb_scales[:, t * P : (t + 1) * P],
                         rhs=moving[a].bitcast(FP8X4),
-                        rhs_scale=[truck_scales, truck_scales1][a][:, cols],
+                        rhs_scale=truck_scales[a][:, cols],
                         start=(a == 0),
                         stop=(a == PASSES - 1),
                     )
                 truck[h, t] = held([P, HALF], F32, f"truck{h}_{t}")
                 nc.scalar.activation(out=truck[h, t][:], in_=acc[:], func=ACT.Sin)
 
-        def make_z(h, on_vector):
+        def gain_on_vector(dst, src, column):
+            nc.vector.tensor_scalar(dst, src, column, None, ALU.mult)
+
+        def gain_on_scalar(dst, src, column):
+            nc.scalar.activation(out=dst, in_=src, func=ACT.Copy, scale=column)
+
+        def make_z(h, apply_gain, copy):
             planar = held([P, PACK, HALF], BF16, f"z_planar{h}")
             grouped = held([P, PACK * HALF], BF16, f"z_grouped{h}")
 
@@ -178,60 +204,53 @@ def tile_list_freight_match_listing_kernel(
                 nc.vector.tensor_tensor(ship[h, t][:], ship[h, t][:], truck[h, t][:], ALU.min)
 
             def gained(t):
-                if on_vector:
-                    nc.vector.tensor_scalar(planar[:, t, :], ship[h, t][:], gain_col[:, t : t + 1], None, ALU.mult)
-                else:
-                    nc.scalar.activation(
-                        out=planar[:, t, :], in_=ship[h, t][:], func=ACT.Copy, scale=gain_col[:, t : t + 1]
-                    )
+                apply_gain(planar[:, t, :], ship[h, t][:], gain_col[:, t : t + 1])
 
             smaller(0)
             for t in range(1, PACK):
                 smaller(t)
                 gained(t - 1)
             gained(PACK - 1)
-            dst = grouped[:].rearrange("p (c i t) -> p c t i", i=4, t=PACK)
-            src = planar[:].rearrange("p t (c i) -> p c t i", i=4)
-            if on_vector:
-                nc.vector.tensor_copy(out=dst, in_=src)
-            else:
-                nc.scalar.copy(out=dst, in_=src)
+            interleave(copy, grouped, planar)
             return grouped
 
-        wb_q = [quantise(round_wb(a), H, f"wb{a}") for a in range(PASSES)]
+        wb_q = [quantise(round_wb(0, nc.scalar.copy), H, "wb0")]
+        gather_pass1(0)
+        wb_q.append(quantise(round_wb(1, nc.vector.tensor_copy), H, "wb1"))
+
         wc_raw = held([P, PACK, N], F32, "wc_raw", "wb_raw0")
         nc.sync.dma_start(out=wc_raw[:], in_=wc.rearrange("(p j) c -> p j c", j=PACK))
         wgo_sb = held([P, S], F32, "wgo_sb", "wb_grouped0")
         nc.sync.dma_start(out=wgo_sb[:], in_=wgo)
         lane_sb = []
-        for n, tag in enumerate(["scale_window", "word_window0", "wb_raw1", "wb_grouped1"]):
-            lane_sb.append(held([P, S], F32, f"lane{n}", tag))
+        for n, reuse in enumerate(["scale_window", "wa_raw", "word_window0", "wb_raw1"]):
+            lane_sb.append(held([P, S], F32, f"lane{n}", reuse))
             nc.sync.dma_start(out=lane_sb[n][:], in_=lane[n * P : (n + 1) * P, :])
-        for h in range(HALVES):
-            gather_pass1(h)
+        gather_pass1(1, "wb_grouped1")
+
         ship_half(0)
-        truck_half(0, wb_q)
+        truck_half(0)
         wc_grouped = held([P, PACK * N], BF16, "wc_grouped")
-        nc.scalar.copy(
-            out=wc_grouped[:].rearrange("p (c i j) -> p c j i", i=4, j=PACK),
-            in_=wc_raw[:].rearrange("p j (c i) -> p c j i", i=4),
-        )
-        truck_half(1, wb_q)
+        interleave(nc.scalar.copy, wc_grouped, wc_raw)
+        truck_half(1)
         ship_half(1)
-        z0 = make_z(0, True)
+
+        z_grouped0 = make_z(0, gain_on_vector, nc.vector.tensor_copy)
         wc_codes, wc_scales = quantise(wc_grouped, N, "wc")
-        z_q = {0: quantise(z0, HALF, "z0")}
-        z1 = make_z(1, False)
+        z_q = {0: quantise(z_grouped0, HALF, "z0")}
+        pages[PAGES - 1] = cleared_page(PAGES - 1, "z_planar0")
+        z_grouped1 = make_z(1, gain_on_scalar, nc.scalar.copy)
 
         def listing(n, h):
             cols = slice(h * HALF, (h + 1) * HALF)
+            z_codes, z_scales = z_q[h]
             acc = psum.tile([P, HALF], F32, name="acc")
             nc.tensor.matmul_mx(
                 out=acc[:],
                 lhsT=wc_codes[:, n * P : (n + 1) * P].bitcast(FP8X4),
                 lhsT_scale=wc_scales[:, n * P : (n + 1) * P],
-                rhs=z_q[h][0][:].bitcast(FP8X4),
-                rhs_scale=z_q[h][1][:],
+                rhs=z_codes[:].bitcast(FP8X4),
+                rhs_scale=z_scales[:],
                 start=True,
                 stop=True,
             )
@@ -242,19 +261,17 @@ def tile_list_freight_match_listing_kernel(
         def place(n, h, y):
             cols = slice(h * HALF, (h + 1) * HALF)
             page = pages[n % PAGES]
-            nc.vector.tensor_tensor(
-                page[:].indirect(list3[:, 32 * h : 32 * (h + 1)]), y[:], wgo_sb[:, cols], ALU.mult
-            )
-            if (n, h) in last_of_page:
+            nc.vector.tensor_tensor(page[:].indirect(half_of(list3, h)), y[:], wgo_sb[:, cols], ALU.mult)
+            if h == 1:
                 nc.sync.dma_start(out=out[n * P : (n + 1) * P, :], in_=page[:])
 
         steps = [(0, 0), (1, 0), (2, 0), (0, 1), (1, 1), (3, 0), (2, 1), (3, 1)]
-        last_of_page = {(n, 1) for n in range(ROWTILES)}
+        first_of_half1 = (0, 1)
         ahead = listing(*steps[0])
         for i, (n, h) in enumerate(steps):
             y = ahead
             if i + 1 < len(steps):
-                if steps[i + 1] == (0, 1):
-                    z_q[1] = quantise(z1, HALF, "z1")
+                if steps[i + 1] == first_of_half1:
+                    z_q[1] = quantise(z_grouped1, HALF, "z1")
                 ahead = listing(*steps[i + 1])
             place(n, h, y)

from contextlib import ExitStack

import concourse.mybir as mybir

K, H, N, T, S, T2 = 1024, 512, 512, 4096, 1024, 2048
FLOPS = 2 * (2 * K * H * S + H * N * S)

F32 = mybir.dt.float32
BF16 = mybir.dt.bfloat16
I32 = mybir.dt.int32
U32 = mybir.dt.uint32
U16 = mybir.dt.uint16
U8 = mybir.dt.uint8
FP8X4 = mybir.dt.float8_e4m3fn_x4
FP4X4 = mybir.dt.float4_e2m1fn_x4
ALU = mybir.AluOpType
ACT = mybir.ActivationFunctionType

P = 128
PACK = 4
PASSES = K // (P * PACK)
QUADRANTS = 4
HALF = S // 2
HALF_LIST = HALF // 16
ROW_TILES = N // P
PAGES = 3
PASS_SHIFT = 16
FIRST_WORDS = 1024
RUN = 4


def tile_list_freight_match_listing_kernel(
    tc, tab_words, tab_scales, offs, offs2, offs3, wa_words, wa_scales, wb, gain, wc, lane, wgo, out
):
    nc = tc.nc
    with ExitStack() as ctx:
        keep = ctx.enter_context(tc.tile_pool(name="keep", bufs=1))
        ring = ctx.enter_context(tc.tile_pool(name="ring", bufs=3))
        psum = ctx.enter_context(tc.psum_pool(name="psum", bufs=8))

        def held(shape, dtype, name, reuse=None):
            return keep.tile(shape, dtype, name=name, tag=reuse or name, align_bytes=64)

        def half_of(list_tile, h):
            return list_tile[:, HALF_LIST * h : HALF_LIST * (h + 1)]

        def cleared_page(i, reuse=None):
            page = held([P, T2], F32, f"page{i}", reuse)
            nc.vector.memset(page[:].bitcast(I32), 0)
            return page

        list1 = held([P, S // 16], U16, "list1")
        list2 = held([P, S // 16], U16, "list2")
        list3 = held([P, S // 16], U16, "list3")
        scale_window = held([P, T], U8, "scale_window")
        word_window = [held([P, T], U32, f"word_window{a}") for a in range(PASSES)]
        wa_scale_raw = held([P, PASSES * H], U8, "wa_scale_raw")
        ship_scales1 = held([P, S], U8, "ship_scales1")
        truck_scales1 = held([P, S], U8, "truck_scales1")

        nc.vector.memset(scale_window[:].bitcast(I32), 0)
        nc.vector.memset(wa_scale_raw[:].bitcast(I32), 0)
        nc.vector.memset(ship_scales1[96:P, :].bitcast(I32), 0)
        nc.vector.memset(truck_scales1[96:P, :].bitcast(I32), 0)

        words_hbm = [tab_words[a].rearrange("p t i -> p (t i)").bitcast(I32) for a in range(PASSES)]
        nc.sync.dma_start(list1[:], offs)
        nc.sync.dma_start(out=word_window[0][:, 0:FIRST_WORDS].bitcast(I32), in_=words_hbm[0][:, 0:FIRST_WORDS])
        scale_rows = tab_scales.rearrange("a (q r) t -> r q a t", r=4)
        for r in range(4):
            nc.sync.dma_start(out=scale_window[r:P:PASS_SHIFT, :].bitcast(I32), in_=scale_rows[r].bitcast(I32))
        nc.sync.dma_start(list2[:], offs2)
        nc.sync.dma_start(out=word_window[0][:, FIRST_WORDS:T].bitcast(I32), in_=words_hbm[0][:, FIRST_WORDS:T])

        pages = {i: cleared_page(i) for i in range(PAGES - 1)}

        wa_raw = held([P, PASSES, 2 * H], U8, "wa_raw")
        for q in range(QUADRANTS):
            nc.sync.dma_start(
                out=wa_scale_raw[32 * q : 32 * q + 4, :].rearrange("r (a c) -> r a c", a=PASSES).bitcast(I32),
                in_=wa_scales[:, 4 * q : 4 * q + 4, :].rearrange("a r c -> r a c").bitcast(I32),
            )
        nc.sync.dma_start(out=wa_raw[:].bitcast(I32), in_=wa_words.rearrange("a p c -> p a c").bitcast(I32))
        wb_raw = [held([P, PACK, H], F32, f"wb_raw{a}") for a in range(PASSES)]
        wb_rows = wb.rearrange("(a p j) c -> a p j c", a=PASSES, j=PACK)
        nc.sync.dma_start(out=wb_raw[0][:], in_=wb_rows[0])
        nc.sync.dma_start(out=word_window[1][:].bitcast(I32), in_=words_hbm[1])

        wa_dealt = held([P, PASSES * 2 * H], U8, "wa_dealt")
        nc.scalar.copy(
            out=wa_dealt[:].bitcast(U16).rearrange("p (a t m) -> p a t m", a=PASSES, t=PACK),
            in_=wa_raw[:].bitcast(U16).rearrange("p a (m t) -> p a t m", t=PACK),
        )

        ship_scales0 = held([P, S], U8, "ship_scales0")
        truck_scales0 = held([P, S], U8, "truck_scales0")
        nc.vector.tensor_copy(ship_scales0[:], scale_window[:].indirect(list1[:]))
        nc.vector.tensor_copy(truck_scales0[:], scale_window[:].indirect(list2[:]))
        for both_passes, pass1 in ((ship_scales0, ship_scales1), (truck_scales0, truck_scales1)):
            nc.sync.dma_start(
                out=pass1[0 : P - PASS_SHIFT, :].bitcast(I32), in_=both_passes[PASS_SHIFT:P, :].bitcast(I32)
            )
        ship_scales = [ship_scales0, ship_scales1]
        truck_scales = [truck_scales0, truck_scales1]

        nc.sync.dma_start(out=wb_raw[1][:], in_=wb_rows[1])
        gain_col = held([P, PACK], F32, "gain_col")
        nc.sync.dma_start(out=gain_col[:], in_=gain.rearrange("(p t) -> p t", t=PACK))
        nc.sync.dma_start(list3[:], offs3)

        ship_words0 = held([P, S], U32, "ship_words0")
        truck_words0 = held([P, S], U32, "truck_words0")
        nc.vector.tensor_copy(ship_words0[:], word_window[0][:].indirect(list1[:]))
        nc.vector.tensor_copy(truck_words0[:], word_window[0][:].indirect(list2[:]))

        wa_scale = held([P, PASSES * H], U8, "wa_scale")
        nc.vector.tensor_copy(
            out=wa_scale[:].rearrange("p (a t m) -> p a t m", a=PASSES, t=PACK),
            in_=wa_scale_raw[:].rearrange("p (a m t) -> p a t m", a=PASSES, t=PACK),
        )

        ship_words1 = []
        truck_words1 = []

        def gather_pass1(h, reuse=None):
            both_lists = held([P, 2 * HALF], U32, f"words1_{h}", reuse)
            ship_words1.append(both_lists[:, 0:HALF])
            truck_words1.append(both_lists[:, HALF : 2 * HALF])
            nc.vector.tensor_copy(ship_words1[h], word_window[1][:].indirect(half_of(list1, h)))
            nc.vector.tensor_copy(truck_words1[h], word_window[1][:].indirect(half_of(list2, h)))

        def quantise(grouped, width, name):
            codes = held([P, width], U32, name + "_codes")
            scales = held([P, width], U8, name + "_scales")
            nc.vector.quantize_mx(out=codes[:].bitcast(FP8X4), scales=scales[:], in_=grouped[:])
            return codes, scales

        def round_wb(a, copy):
            grouped = held([P, PACK * H], BF16, f"wb_grouped{a}")
            copy(
                out=grouped[:].rearrange("p (t m j) -> p m t j", t=PACK, j=PACK),
                in_=wb_raw[a][:].rearrange("p j (m t) -> p m t j", t=PACK),
            )
            return grouped

        def interleave(copy, grouped, planar):
            copy(
                out=grouped[:].rearrange("p (c i j) -> p c j i", i=RUN, j=PACK),
                in_=planar[:].rearrange("p j (c i) -> p c j i", i=RUN),
            )

        ship = {}
        truck = {}

        def ship_half(h):
            cols = slice(h * HALF, (h + 1) * HALF)
            moving = [ship_words0[:, cols], ship_words1[h]]
            for t in range(PACK):
                acc = psum.tile([P, HALF], F32, name="acc")
                for a in range(PASSES):
                    c0 = a * H + t * P
                    nc.tensor.matmul_mx(
                        out=acc[:],
                        lhsT=wa_dealt[:, 2 * c0 : 2 * (c0 + P)].bitcast(FP4X4),
                        lhsT_scale=wa_scale[:, c0 : c0 + P],
                        rhs=moving[a].bitcast(FP8X4),
                        rhs_scale=ship_scales[a][:, cols],
                        start=(a == 0),
                        stop=(a == PASSES - 1),
                    )
                ship[h, t] = held([P, HALF], F32, f"ship{h}_{t}")
                nc.scalar.activation(out=ship[h, t][:], in_=acc[:], func=ACT.Tanh)

        def truck_half(h):
            cols = slice(h * HALF, (h + 1) * HALF)
            moving = [truck_words0[:, cols], truck_words1[h]]
            for t in range(PACK):
                acc = psum.tile([P, HALF], F32, name="acc")
                for a in range(PASSES):
                    wb_codes, wb_scales = wb_q[a]
                    nc.tensor.matmul_mx(
                        out=acc[:],
                        lhsT=wb_codes[:, t * P : (t + 1) * P].bitcast(FP8X4),
                        lhsT_scale=wb_scales[:, t * P : (t + 1) * P],
                        rhs=moving[a].bitcast(FP8X4),
                        rhs_scale=truck_scales[a][:, cols],
                        start=(a == 0),
                        stop=(a == PASSES - 1),
                    )
                truck[h, t] = held([P, HALF], F32, f"truck{h}_{t}")
                nc.scalar.activation(out=truck[h, t][:], in_=acc[:], func=ACT.Sin)

        def gain_on_vector(dst, src, column):
            nc.vector.tensor_scalar(dst, src, column, None, ALU.mult)

        def gain_on_scalar(dst, src, column):
            nc.scalar.activation(out=dst, in_=src, func=ACT.Copy, scale=column)

        def make_z(h, apply_gain, copy):
            planar = held([P, PACK, HALF], BF16, f"z_planar{h}")
            grouped = held([P, PACK * HALF], BF16, f"z_grouped{h}")

            def smaller(t):
                nc.vector.tensor_tensor(ship[h, t][:], ship[h, t][:], truck[h, t][:], ALU.min)

            def gained(t):
                apply_gain(planar[:, t, :], ship[h, t][:], gain_col[:, t : t + 1])

            smaller(0)
            for t in range(1, PACK):
                smaller(t)
                gained(t - 1)
            gained(PACK - 1)
            interleave(copy, grouped, planar)
            return grouped

        wb_q = [quantise(round_wb(0, nc.scalar.copy), H, "wb0")]
        gather_pass1(0)
        wb_q.append(quantise(round_wb(1, nc.vector.tensor_copy), H, "wb1"))

        wc_raw = held([P, PACK, N], F32, "wc_raw", "wb_raw0")
        nc.sync.dma_start(out=wc_raw[:], in_=wc.rearrange("(p j) c -> p j c", j=PACK))
        wgo_sb = held([P, S], F32, "wgo_sb", "wb_grouped0")
        nc.sync.dma_start(out=wgo_sb[:], in_=wgo)
        lane_sb = []
        for n, reuse in enumerate(["scale_window", "wa_raw", "word_window0", "wb_raw1"]):
            lane_sb.append(held([P, S], F32, f"lane{n}", reuse))
            nc.sync.dma_start(out=lane_sb[n][:], in_=lane[n * P : (n + 1) * P, :])
        gather_pass1(1, "wb_grouped1")

        ship_half(0)
        truck_half(0)
        wc_grouped = held([P, PACK * N], BF16, "wc_grouped")
        interleave(nc.scalar.copy, wc_grouped, wc_raw)
        truck_half(1)
        ship_half(1)

        z_grouped0 = make_z(0, gain_on_vector, nc.vector.tensor_copy)
        wc_codes, wc_scales = quantise(wc_grouped, N, "wc")
        z_q = {0: quantise(z_grouped0, HALF, "z0")}
        pages[PAGES - 1] = cleared_page(PAGES - 1, "z_planar0")
        z_grouped1 = make_z(1, gain_on_scalar, nc.scalar.copy)

        def listing(n, h):
            cols = slice(h * HALF, (h + 1) * HALF)
            z_codes, z_scales = z_q[h]
            acc = psum.tile([P, HALF], F32, name="acc")
            nc.tensor.matmul_mx(
                out=acc[:],
                lhsT=wc_codes[:, n * P : (n + 1) * P].bitcast(FP8X4),
                lhsT_scale=wc_scales[:, n * P : (n + 1) * P],
                rhs=z_codes[:].bitcast(FP8X4),
                rhs_scale=z_scales[:],
                start=True,
                stop=True,
            )
            y = ring.tile([P, HALF], F32, name="y")
            nc.vector.tensor_tensor(y[:], acc[:], lane_sb[n][:, cols], ALU.mult)
            return y

        def place(n, h, y):
            cols = slice(h * HALF, (h + 1) * HALF)
            page = pages[n % PAGES]
            nc.vector.tensor_tensor(page[:].indirect(half_of(list3, h)), y[:], wgo_sb[:, cols], ALU.mult)
            if h == 1:
                nc.sync.dma_start(out=out[n * P : (n + 1) * P, :], in_=page[:])

        steps = [(0, 0), (1, 0), (2, 0), (0, 1), (1, 1), (3, 0), (2, 1), (3, 1)]
        first_of_half1 = (0, 1)
        ahead = listing(*steps[0])
        for i, (n, h) in enumerate(steps):
            y = ahead
            if i + 1 < len(steps):
                if steps[i + 1] == first_of_half1:
                    z_q[1] = quantise(z_grouped1, HALF, "z1")
                ahead = listing(*steps[i + 1])
            place(n, h, y)
